import numpy as np, ml_dtypes
CORES = [66,74,82,90,194,202,210,218]
N = 8
import mx_ref
BF = ml_dtypes.bfloat16
def gentries(a):
    return np.ascontiguousarray(a.reshape(8, 16, -1).transpose(0, 2, 1)).reshape(8, -1)
def gtable(e):
    e = np.asarray(e); return np.ascontiguousarray(e.reshape(8, -1, 16).transpose(0, 2, 1)).reshape(128, -1).astype(np.int32)
def gcols(t, e):
    v = np.concatenate([t.reshape(8, 16, -1, 4), np.zeros((8, 16, 1, 4), BF)], axis=2)
    return np.ascontiguousarray(np.stack([v[g][:, e[g]] for g in range(8)])).reshape(128, -1)
def pick(q, e):
    c = np.concatenate([q[0].reshape(128, -1, 4), np.zeros((128, 1, 4), np.uint8)], axis=1); s = np.concatenate([q[1], np.ones((16, 1), np.uint8)], axis=1)
    return (np.ascontiguousarray(c[:, e].reshape(128, -1)), np.ascontiguousarray(s[:, e]))
def join(*qs):
    return (np.concatenate([q[0] for q in qs], axis=1), np.concatenate([q[1] for q in qs], axis=1))
def put(q, e, v):
    c, s = q[0].reshape(128, -1, 4).copy(), q[1].copy(); c[:, e] = v[0].reshape(128, -1, 4); s[:, e] = v[1]
    return (c.reshape(128, -1), s)
def pk(c, s):
    return (np.ascontiguousarray(c), mx_ref.live(s))
def emit(q):
    return q[0], q[1]
def packed(v, rng):
    q = [mx_ref.quantize(np.ascontiguousarray(v[r])) for r in range(N)]
    return np.stack([a for a, b in q]), np.stack([mx_ref.plane(b, rng) for a, b in q])
def values_of_codes():
    e, c = np.zeros((128, 128, 4), np.float32), np.zeros((128, 2, 4), np.uint8)
    e[np.arange(128), np.arange(128), 0] = 1
    c[:127, :, 0] = np.arange(256).reshape(2, 128).T[:127]
    return mx_ref.matmul(mx_ref.quantize(e.reshape(128, 512).astype(BF)), (c.reshape(128, 8), np.full((16, 2), 127, np.uint8))).T.reshape(-1).astype(np.float64)
CODE_VALUE, SCALE_VALUE = values_of_codes(), 2.0 ** (np.arange(256) - 127.0)
def decode(q):
    return (CODE_VALUE[q[0]].reshape(16, 8, -1, 4) * SCALE_VALUE[q[1]][:, None, :, None] + 0.0).reshape(128, -1).astype(np.float32)
def f(rng, *shape):
    return mx_ref.flush((rng.standard_normal(shape, dtype=np.float32) * np.exp2(rng.integers(-2, 3, shape[:-1] + (1,)))).astype(BF))
def wide(rng, *shape, cols=0):
    v = rng.standard_normal(shape, dtype=np.float32) * np.exp2(rng.integers(-12, 13, shape)).astype(np.float32)
    if cols: v *= np.repeat(np.exp2(rng.integers(-cols, cols + 1, shape[:-2] + (1, shape[-1] // 4))) * (rng.random(shape[:-2] + (1, shape[-1] // 4)) > 0.0625), 4, axis=-1).astype(np.float32)
    return mx_ref.flush(v.astype(BF))
C, M, R = 320, 128, 3
def numbers_of(rng):
    return {"x": np.array(f(rng, N, 128, 4 * C)), "u": np.array(f(rng, N, 128, 512)), "v": np.array(f(rng, N, 128, 512))}
def shuffled(rng):
    return np.argsort(rng.random((N, 8, C)), axis=2)
def stored(t):
    return {"cf": np.stack([gtable(t[r]) for r in range(N)])}
def weights(rng, w):
    c, p = packed(np.ascontiguousarray(w).reshape(N, 128, 2048), rng)
    return {"wc": c, "ws": p}
def layers(rng, still=[]):
    w = np.array(f(rng, N, 128, 2048)).reshape(N, 8, 16, 4, 8, 16, 4)
    for i in still:
        w[:, :, i] = 0
        w[:, :, :, :, :, i] = 0
    return weights(rng, w)
def setup_inputs(rng):
    return {**numbers_of(rng), **stored(shuffled(rng)), **layers(rng)}
def setup_inputs_ties(rng):
    d = numbers_of(rng)
    x = d["x"].reshape(N, 8, 16, C, 4)
    x[:, :, :2] = 0
    x[:, :, 0, :, 0] = rng.integers(0, 4, (N, 8, C)).astype(np.float32).astype(BF)
    x[:, :, 1, :, 0] = rng.integers(0, 3, (N, 8, C)).astype(np.float32).astype(BF)
    u = d["u"].reshape(N, 128, 128, 4)
    u[:, :, ::16] = 0
    u[:, :, 1] = 0
    o = rng.permutation(N)
    for r in range(N):
        s = 0.0 if r == o[0] else -1.0 if r == o[1] else 1.0
        for h in range(0, 128, 16): u[r, h, h, 0] = s
        u[r, 1, 1, 0] = s
    return {"x": x.reshape(N, 128, 4 * C), "u": u.reshape(N, 128, 512), "v": d["v"], **stored(shuffled(rng)), **layers(rng, [0, 1])}
def setup_inputs_near(rng):
    d = numbers_of(rng)
    o = rng.permutation(N) % 4
    c = np.where(o % 2 == 0, 1.0, -1.0)
    x = d["x"].astype(np.float32).reshape(N, 8, 16, C, 4)
    x[:, :, 0] = 0
    x[:, :, 8:] = 0
    x[:, :, 0, :, 0] = c[:, None, None]
    s = rng.integers(0, 16, (N, 8, C))
    x[:, :, 8] = ((s[:, :, :, None] >> np.arange(4)) & 1) * np.exp2(np.arange(4) - 23.0)
    x[:, :, 11, :, 0] = 2.0 ** -10
    u = d["u"].reshape(N, 128, 128, 4)
    u[:, :, ::16] = 0
    u[:, :, 1] = 0
    for r in range(N):
        for g in 1 + rng.permutation(7)[:4]: x[r, g, 0, rng.integers(C), 0] = c[r] * 2.0 ** 29
        if o[r] == 1: x[r, 0, 0, rng.integers(C), 0] = -2.0 ** 29
        if o[r] == 3:
            i = rng.integers(0, 2, (8, C))
            x[r, :, 8:] = 0
            x[r, :, 10, :, 0] = (1.0 + 0.125 * i) * 2.0 ** -30
            x[r, :, 12, :, 0] = (1.125 - 0.125 * i) * 2.0 ** -30
        k = 2.0 ** -30 if o[r] == 2 else 1.0
        for a, h in [(0, 1)] + [(h, h) for h in range(0, 128, 16)]:
            if o[r] == 3:
                u[r, a + 10, h, 0] = 1.125 * 2.0 ** -30
                u[r, a + 12, h, 0] = 2.0 ** -30
            else:
                u[r, a, h, 0] = k
                u[r, a + 8, h] = k
                u[r, a + 11, h, 0] = k
    return {"x": x.reshape(N, 128, 4 * C).astype(BF), "u": u.reshape(N, 128, 512), "v": d["v"], **stored(shuffled(rng)), **layers(rng, [0] + [8, 9, 10, 11, 12, 13, 14, 15])}
def swings(rng):
    h, j, a = np.zeros(C, int), 0, 200
    while j < C:
        i = np.arange(min(int(rng.integers(10, 25)), C - j))
        n = np.where((i > 8) & (rng.random(len(i)) < 0.25), rng.integers(2, np.maximum(i, 3)), i)
        h[j:j + len(i)] = (1 - 2 * (i % 2)) * (a - 8 * n)
        j, a = j + len(i), a + 1
    return h
def setup_inputs_deep(rng):
    d = numbers_of(rng)
    x = d["x"].reshape(N, 8, 16, C, 4)
    o = rng.permutation(N)
    t = np.arange(C) - C // 2
    small = (1.0 + (2 * rng.integers(0, 64, (N, 8, 8, C, 4)) + 1) * 2.0 ** -7) * np.exp2(-rng.integers(8, 15, (N, 8, 8, C, 4)).astype(np.float64))
    small = small * rng.choice([-1.0, 1.0], small.shape)
    small[:, :, 0, :, 0] = np.where(rng.random((N, 8, C)) < 0.5, 1.875, 1.96875)
    x[:, :, 8:] = small.astype(np.float32).astype(BF)
    x[:, 0, 0] = 0
    u = d["u"].reshape(N, 128, 128, 4)
    u[:, :, 1] = 0
    u[:, 0, 1, 0] = 16
    u[:, 0, 1, 1] = 1
    for r in range(N):
        h = t if r == o[0] else -t if r == o[1] else swings(rng)
        x[r, 0, 0, :, 0] = (np.sign(h) * (np.abs(h) // 16)).astype(np.float32).astype(BF)
        x[r, 0, 0, :, 1] = (np.sign(h) * (np.abs(h) % 16)).astype(np.float32).astype(BF)
    return {"x": x.reshape(N, 128, 4 * C), "u": u.reshape(N, 128, 512), "v": d["v"], **stored(shuffled(rng)), **layers(rng)}
def setup_inputs_ends(rng):
    d = numbers_of(rng)
    o = (np.arange(N) + int(rng.integers(N))) % 4
    x = np.zeros((N, 8, 16, C, 4))
    u = d["u"].reshape(N, 128, 128, 4)
    u[:, :, ::16] = 0
    t = shuffled(rng)
    w = np.zeros((N, 128, 4, 128, 4), np.float32)
    i = np.arange(128)
    for r in range(N):
        sign = rng.permutation(8) % 2 * 2.0 - 1.0
        wave = 2.0 ** 30 * (0.9 + 0.1 * rng.random((128, 8, 4)))
        u[r, :, 1] = 2.0 ** -30 if o[r] == 3 else 2.0 ** 30
        if o[r] == 0:
            x[r] = -2.0 ** 30 * (0.9 + 0.1 * rng.random((8, 16, C, 4)))
            u[r, :, ::16] = wave.astype(np.float32).astype(BF)
            t[r] = np.arange(C)
        if o[r] == 1:
            x[r] = 2.0 ** 30 * np.where(rng.random((8, 16, C, 4)) < 0.125, 0.8125, 0.875) * (rng.permutation(C) % 2 * 2.0 - 1.0)[:, None]
            u[r, :, ::16] = (wave * sign[:, None]).astype(np.float32).astype(BF)
            for b in range(4): w[r, i, b, i, b] = rng.choice([-1.0, 1.0], 128)
        if o[r] == 2:
            x[r] = 2.0 ** 30
            x[r, rng.permutation(8)[:4]] *= np.where(rng.random((4, 1, C, 1)) < 0.5, 0.875, 1.0)
            t[r] = np.arange(C)[::-1]
            for g in range(8): u[r, 16 * g:16 * g + 16, 16 * g] = sign[g] * 2.0 ** 30
        if o[r] == 3:
            x[r] = 2.0 ** -30 * (1.0 + 0.125 * rng.integers(0, 8, (8, 16, C, 4)))
            t[r, ::2] = np.arange(C)
            t[r, 1::2] = np.arange(C)[::-1]
            for g in range(8): u[r, 16 * g:16 * g + 16, 16 * g] = 2.0 ** -30
    d["v"] = (np.where(d["v"] < 0, -1.0, 1.0) * np.where(rng.permutation(N) % 2, 2.0 ** -30, 2.0 ** 30)[:, None, None]).astype(np.float32).astype(BF)
    return {"x": x.astype(np.float32).reshape(N, 128, 4 * C).astype(BF), "u": u.reshape(N, 128, 512), "v": d["v"], **stored(t), **weights(rng, w.astype(BF))}
def setup_inputs_spread(rng):
    d = setup_inputs(rng)
    d["x"] = wide(rng, N, 128, 4 * C, cols=6)
    return d
def check_inputs(d):
    b = []
    for k in ("x", "u", "v"):
        a = np.abs(d[k].astype(np.float32))
        if not (np.isfinite(a).all() and ((a == 0) | (a >= 2.0 ** -30) & (a <= 2.0 ** 30)).all()): b.append("a value of " + k)
    none, least, most = [emit(mx_ref.quantize(np.full((128, 16), k, np.float32).astype(BF)))[1][0, 0] for k in (0.0, 2.0 ** -30, 2.0 ** 30)]
    for r in range(N):
        if (np.sort(gentries(d["cf"][r]), axis=1) != np.arange(C)).any(): b.append("cf: a group hasn't every column once")
        if ((d["wc"][r] == 0x7F) | (d["wc"][r] == 0xFF)).any(): b.append("wc: a code that is no number")
        s = mx_ref.live(d["ws"][r])
        if ((s != none) & ((s < least) | (s > most))).any(): b.append("ws: a scale out of range")
    return b
def turning(h):
    t = np.arange(C)
    e, found = np.zeros(C, np.int64), []
    for i in range(7):
        inside = (t >= e[:, None]) & (t <= t[:, None])
        s = np.where(inside, h if i % 2 == 0 else -h, np.float32(-np.inf))
        e = C - 1 - np.argmax(s[:, ::-1], axis=1)
        found.append(e)
    found = np.stack(found + [t])
    return found, np.argmax(found == t, axis=0)
def reference(x, u, v, cf, wc, ws):
    qu = [mx_ref.quantize(u[r]) for r in range(N)]
    lay = [pk(wc[r], ws[r]) for r in range(N)]
    now = [x[r] for r in range(N)]
    reads = [gentries(cf[r]) for r in range(N)]
    for t in range(R):
        blend, low, sent = [], [], []
        for r in range(N):
            q = mx_ref.quantize(now[r])
            own = decode(q).astype(BF)
            s = mx_ref.matmul(qu[r], q) + np.float32(0.0)
            e, depth = turning(s[1])
            at = np.take_along_axis(e, np.maximum(depth - np.arange(9)[:, None], 0), axis=0)
            a = np.take_along_axis(reads[r], at[:8], axis=1)
            b = np.take_along_axis(reads[r], at[1:], axis=1)
            z = ((gcols(own, a).astype(np.float32) + gcols(own, b).astype(np.float32)) * np.float32(0.5)).astype(BF)
            o = np.argsort(-s[::16], axis=1, kind="stable")
            l, d = o[:, :M], o[:, C - M:]
            sent.append(mx_ref.quantize(gcols(z, l)))
            other = np.tile(np.arange(C), (8, 1))
            np.put_along_axis(other, l, d, axis=1)
            np.put_along_axis(other, d, l, axis=1)
            reads[r] = np.take_along_axis(other, reads[r], axis=1)
            blend.append(z)
            low.append(d)
        for r in range(N):
            came = sent[(r - 1) % N]
            made = np.stack([mx_ref.matmul(pick(lay[r], np.arange(128 * b, 128 * b + 128)), came) * np.float32(0.03125) for b in range(4)], axis=2).reshape(8, 16, M, 4)
            z = blend[r].astype(np.float32).reshape(8, 16, C, 4)
            for g in range(8): z[g][:, low[r][g]] = made[g] + z[g][:, low[r][g]]
            now[r] = z.reshape(128, 4 * C).astype(BF)
    y, op = np.zeros((N, 128, C), np.float32), np.zeros((N, 8, C), np.float32)
    oc, osc = np.zeros((N, 128, 4 * C), np.uint8), np.zeros((N, 16, C), np.uint8)
    for r in range(N):
        q = mx_ref.quantize(now[r])
        y[r] = mx_ref.matmul(mx_ref.quantize(v[r]), q)
        op[r] = reads[r]
        oc[r], osc[r] = emit(q)
    return {"y": y, "op": op, "oc": oc, "osc": osc}

from concourse.mybir import dt, AluOpType as A, ActivationFunctionType as AF

ROUNDS = 3
BIG = 2.0 ** 81
HUGE = 2.0 ** 90
VECTOR_KS = 8

SCRATCH = {}
for _t, _names in {
    "bfloat16": "xt 1280 ut 512 vt 512 ones 520 unit 520 jm 320 tt 320 m2a 320 m2 320 res 320 keep 320 zer 320 msa 320 msb 320 msc 320 "
                "ms 320 j8 160 eq 320 ec 320 cmp 6400 junk 6400 dif 2240 dd 2240 ev 2240 sv 2240 el 160 nf 336 pen 192 pa 320 pb 160 "
                "pc 80 pd 40 fb 1280 fl 1280 ga 1280 zp 1280 et 512 ord 320 lm 128 lsx 128 ords 320 pi 320 cm 320 cs 320",
    "float32": "pif 1 pgf 1 pg20 1 pi2 1 ja 160 lstf 12 hn 320 cc 640 ab 320 sha 320 sh 320 rs 20 rk 20 mm 2240 opl 320 rp 544 yt 320",
    "int32": "cfi 20 pidx 8 pand 8 pshr 8 lsti 12 osi 8",
    "uint16": "lst 12 offs 8 offh 8 rk16 20 ro16 20 oab 40 l16 8 cw16 20",
    "float8_e4m3fn_x4": "wq 512 uq 128 vq 128 usq 128 uhq 128 xq 320 ebq 512 eq0 128 eq1 128 eq2 128 aq0 128 aq1 128 aq2 128",
    "uint8": "wsp 512 us 128 vs 128 uss 128 uhs 128 xs 320 ebs 512 es0 128 es1 128 es2 128 as0 128 as1 128 as2 128",
}.items():
    _w = _names.split()
    for _n, _c in zip(_w[::2], _w[1::2]):
        SCRATCH[_n] = ("sbuf", [128, int(_c)], _t)
for _n in ("ph", "ps1", "ps2", "pf0", "pf1", "pf2", "pf3", "py"):
    SCRATCH[_n] = ("psum", [128, 512], "float32")

SEMAPHORES = ["cv", "cs", "ct", "cg", "dx", "du", "dv", "dc", "dwa", "dwb", "out1", "out2", "loc", "arr0", "arr1", "arr2"]


def rank_program(g, core, T, topo):
    rank = T.rank_of(core)
    if rank is None:
        return
    nxt = T.cores[(rank + 1) % len(T.cores)]
    rid, pid = topo.addr(nxt, core)
    mask = topo.mask(core, nxt)
    eng = {"v": g.vector, "s": g.scalar, "t": g.tensor, "g": g, "y": g.sync}
    known = {q: {} for q in eng}
    count, writer, readers = {}, {}, {}

    def before(q, reads, writes):
        deps = [writer[k] for k in list(reads) + list(writes) if k in writer]
        for k in writes:
            deps += readers.get(k, [])
        for s, n, snap in sorted(deps, key=lambda d: -d[1]):
            if known[q].get(s, 0) < n:
                eng[q].wait_ge(T.sem[s], n)
                for a, b in snap.items():
                    if known[q].get(a, 0) < b:
                        known[q][a] = b

    def after(q, s, inc, reads, writes):
        count[s] = count.get(s, 0) + inc
        snap = dict(known[q])
        snap[s] = count[s]
        rec = (s, count[s], snap)
        for k in reads:
            readers.setdefault(k, []).append(rec)
        for k in writes:
            writer[k] = rec
            readers[k] = []

    def op(q, reads, writes, fn, *a, **k):
        before(q, reads, writes)
        fn(*a, **k).then_inc(T.sem["c" + q], 1)
        after(q, "c" + q, 1, reads, writes)

    def dma(q, s, reads, writes, out, in_):
        before(q, reads, writes)
        eng[q].dma_start(out, in_).then_inc(T.sem[s], 16)
        after(q, s, 16, reads, writes)

    V, S, P = g.vector, g.scalar, g.tensor
    ts, tt, sc, cp, act = V.tensor_scalar, V.tensor_tensor, V.tensor_tensor_scan, V.tensor_copy, S.activation

    def blk(t, b, n=320):
        return t[:, n * b:n * b + n]

    def mm(out_key, out, n, wkeys, w, wscale, xkeys, x, xscale):
        op("t", wkeys + xkeys, [out_key], P.matmul_mx, out[:, 0:n], w, wscale, x, xscale, True, True)

    dma("y", "dx", [], ["xt"], T.xt[:], T.x[:])
    dma("s", "du", [], ["ut"], T.ut[:], T.u[:])
    dma("y", "dc", [], ["cfi"], T.cfi[:], T.cf[:])
    dma("s", "dwa", [], ["wq"], T.wq[:, 0:512].bitcast(dt.uint8), T.wc[:, 0:2048])
    dma("y", "dwb", [], ["wsp"], T.wsp[:, 0:512], T.ws[:, 0:512])
    dma("y", "dv", [], ["vt"], T.vt[:], T.v[:])
    inexact = {"allow_small_or_imprecise_dtypes": True}
    op("g", [], ["osi"], g.iota, T.osi[:], [[16, 8]], 0, 0)
    op("g", [], ["pidx"], g.iota, T.pidx[:, 0:1], [[1, 1]], 0, 1)
    op("g", [], ["jm"], g.iota, T.jm[:], [[0, 20], [1, 16]], 0, 0, **inexact)
    op("g", [], ["ja"], g.iota, T.ja[:], [[0, 8], [16, 20]], -160, 0, **inexact)
    op("g", [], ["lsti"], g.iota, T.lsti[:], [[16, 12]], 0, 0)
    op("v", [], ["ones"], V.memset, T.ones[:], 1.0)
    op("g", ["ones"], ["unit"], g.affine_select, T.unit[:], T.ones[:], [[1, 520]], A.is_equal, 0.0, -4, -4)
    op("g", [], ["tt"], g.iota, T.tt[:], [[1, 320]], -160, 0, **inexact)
    op("v", [], ["offh"], V.memset, T.offh[:], 1)
    op("v", ["osi"], ["offs"], cp, T.offs[:], T.osi[:])
    op("v", ["pidx"], ["pand"], ts, T.pand[:, 0:1], T.pidx[:, 0:1], 15, None, A.bitwise_and)
    op("v", ["pidx"], ["pshr"], ts, T.pshr[:, 0:1], T.pidx[:, 0:1], 4, None, A.arith_shift_right)
    op("v", [], ["zer"], V.memset, T.zer[:], 0.0)
    op("v", ["pand"], ["pif"], cp, T.pif[:], T.pand[:, 0:1])
    op("v", ["pshr"], ["pgf"], cp, T.pgf[:], T.pshr[:, 0:1])
    op("v", [], ["nf"], V.memset, T.nf[:], 0.0)
    op("v", ["pif"], ["pi2"], ts, T.pi2[:], T.pif[:], 15.0, None, A.is_lt)
    op("v", ["pgf"], ["pg20"], ts, T.pg20[:], T.pgf[:], 20.0, None, A.mult)
    op("v", ["jm", "pif"], ["m2a"], ts, T.m2a[:], T.jm[:], T.pif[:, 0:1], 2 * HUGE, A.is_equal, A.mult)
    op("v", ["jm"], ["res"], ts, T.res[:], T.jm[:], 0.0, -2 * HUGE, A.is_equal, A.mult)
    op("v", ["m2a"], ["m2"], ts, T.m2[:], T.m2a[:], -HUGE, None, A.add)
    op("v", ["jm"], ["keep"], ts, T.keep[:], T.jm[:], 0.0, None, A.not_equal)
    op("v", ["ut"], ["uq"], V.quantize_mx, T.uq[:, 0:128], T.us[:, 0:128], T.ut[:])
    for o, q, s in (("offs", "usq", "uss"), ("offh", "uhq", "uhs")):
        op("v", ["uq", o], [q], cp, T[q][:, 0:128].bitcast(dt.uint32), T.uq[:, 0:128].bitcast(dt.uint32).indirect(T[o][:, 0:8]))
        op("v", ["uq", o], [s], cp, T[s][:, 0:128], T.us[:, 0:128].indirect(T[o][:, 0:8]))

    def late_constants():
        for b in range(4):
            op("v", ["unit"], ["eb%d" % b], V.quantize_mx, blk(T.ebq, b, 128), blk(T.ebs, b, 128), T.unit[:, 4 - b:516 - b])
        op("v", ["jm", "pif"], ["msa"], ts, T.msa[:], T.jm[:], T.pif[:, 0:1], None, A.is_lt)
        op("v", ["jm", "pi2"], ["msb"], ts, T.msb[:], T.jm[:], 15.0, T.pi2[:, 0:1], A.is_equal, A.mult)
        op("v", ["ja", "pif"], ["j8"], ts, T.j8[:], T.ja[:], T.pif[:, 0:1], None, A.add)
        op("v", ["msa", "msb"], ["msc"], tt, T.msc[:], T.msa[:], T.msb[:], A.add)
        op("v", ["lsti", "pif", "pg20"], ["lstf"], ts, T.lstf[:], T.lsti[:], T.pif[:, 0:1], T.pg20[:, 0:1], A.add, A.add)
        op("v", ["msc"], ["ms"], ts, T.ms[:], T.msc[:], BIG, -0.5 * BIG, A.mult, A.add)
        op("v", ["lstf"], ["lst"], cp, T.lst[:], T.lstf[:])
        op("v", ["j8"], ["el7"], cp, T.el[:, 140:160], T.j8[:, 140:160])
        op("v", ["cfi"], ["cw16"], cp, T.cw16[:], T.cfi[:])

    va, sb = list(range(VECTOR_KS)), list(range(VECTOR_KS, 20))
    pf = [T.pf0, T.pf1, T.pf2, T.pf3]
    h = T.ph[:, 0:320]
    QX = (["xq"], T.xq[:, 0:320], T.xs[:, 0:320])

    def compare(k):
        op("v", ["c0", "c1", "sh"], ["cmp%d" % k], ts, blk(T.cmp, k), T.cc[:, 16 * k + 16:16 * k + 336], T.sh[:, 16 * k + 15:16 * k + 16], None, A.is_gt)

    def sign(k):
        op("s", ["c0", "c1", "sh"], ["cmp%d" % k], act, blk(T.cmp, k), T.cc[:, 16 * k + 16:16 * k + 336], AF.Sign,
           bias=T.sh[:, 16 * k + 15:16 * k + 16], scale=-1.0)

    def total(k, f, s):
        op("s", ["cmp%d" % k], ["rs%d" % k, "jk%d" % k], act, blk(T.junk, k), blk(T.cmp, k), f, scale=s, accum_out=T.rs[:, k:k + 1])

    def hold(i):
        op("v", ["dd%d" % i, "tt"], ["ev%d" % i], sc, blk(T.ev, i), blk(T.dd, i), T.tt[:], 0.0, A.add, A.min)

    def sample(i):
        op("v", ["ev%d" % i, "ms"], ["sv%d" % i], sc, blk(T.sv, i), blk(T.ev, i), T.ms[:], 0.5 * BIG, A.min, A.max)

    for r in range(ROUNDS):
        op("v", ["x0", "x1", "x2", "x3", "xt"], ["xq"], V.quantize_mx, T.xq[:, 0:320], T.xs[:, 0:320], T.xt[:])
        if r == 0:
            late_constants()
            op("v", [], ["rp0", "rp1", "rp2", "rp3"], V.memset, T.rp[:], 0.0)
        mm("ps1", T.ps1, 320, ["usq", "uss"], T.usq[:, 0:128], T.uss[:, 0:128], *QX)
        mm("ph", T.ph, 320, ["uhq", "uhs"], T.uhq[:, 0:128], T.uhs[:, 0:128], *QX)
        mm("ps2", T.ps2, 320, ["usq", "uss"], T.usq[:, 0:128], T.uss[:, 0:128], *QX)
        for b in range(4):
            mm("pf%d" % b, pf[b], 320, ["eb%d" % b], blk(T.ebq, b, 128), blk(T.ebs, b, 128), *QX)

        op("s", [], ["hn", "ph"], act, T.hn[:], h, AF.Copy, scale=-1.0)
        op("s", ["ps2"], ["aa"], act, T.ab[:], T.ps2[:, 0:320], AF.Abs, scale=0.6 * 2.0 ** -23, bias=2.0 ** -124)
        op("s", ["ps2"], ["c0"], act, T.cc[:, 0:320], T.ps2[:, 0:320], AF.Copy)
        for b in range(4):
            op("s", ["pf%d" % b], ["fb%d" % b], act, blk(T.fb, b), pf[b][:, 0:320], AF.Copy, scale=0.5)

        op("v", ["ps1", "m2"], ["sha"], tt, T.sha[:], T.ps1[:, 0:320], T.m2[:], A.min)
        op("v", ["res", "sha"], ["sh"], sc, T.sh[:], T.res[:], T.sha[:], 0.0, A.add, A.max)
        fill = [lambda: op("v", ["aa", "ps1"], ["c1"], tt, T.cc[:, 320:640], T.ab[:], T.ps1[:, 0:320], A.add),
                lambda: op("v", ["sh", "ps1"], ["eqq"], tt, T.eq[:], T.sh[:], T.ps1[:, 0:320], A.is_equal)]
        for k in va:
            fill.append(lambda k=k: compare(k))
        fill.append(lambda: op("v", ["keep", "eqq"], ["ec"], sc, T.ec[:], T.keep[:], T.eq[:], 0.0, A.mult, A.add))

        def filler():
            if fill:
                fill.pop(0)()
        for i in range(7):
            M, K = blk(T.mm, i), "mm%d" % i
            if i == 0:
                op("v", ["zer", "ph"], [K], sc, M, T.zer[:], h, -BIG, A.add, A.max)
            elif i % 2:
                op("v", ["dd%d" % (i - 1), "ph"], [K], sc, M, blk(T.dd, i - 1), h, 0.0, A.add, A.min)
            else:
                op("v", ["dd%d" % (i - 1), "hn"], [K], sc, M, blk(T.dd, i - 1), T.hn[:], 0.0, A.add, A.min)
            filler()
            op("v", [K, "ph"], ["df%d" % i], tt, blk(T.dif, i), M, h, A.add if i % 2 == 0 and i else A.subtract)
            filler()
            op("v", ["df%d" % i], ["dd%d" % i], ts, blk(T.dd, i), blk(T.dif, i), 0.0, BIG, A.is_equal, A.mult)
            filler()
            fill.insert(0, lambda i=i: hold(i))
            fill.insert(min(2, len(fill)), lambda i=i: sample(i))
        while fill:
            filler()

        for n, k in enumerate(sb):
            sign(k)
            if n:
                total(sb[n - 1], AF.Relu, -1.0)
        for b in range(4):
            op("s", ["fb%d" % b, "cw16"], ["fl%d" % b], act, blk(T.fl, b), blk(T.fb, b).indirect(T.cw16[:, 0:20]), AF.Copy)
            if b == 0:
                total(sb[-1], AF.Relu, -1.0)
        for k in va:
            total(k, AF.Copy, 1.0)

        op("v", ["sv%d" % i for i in range(7)], ["el"], tt, T.el[:, 0:140], T.sv[:, 14:2240:16], T.sv[:, 15:2240:16], A.min)
        op("v", ["el", "j8"], ["nf"], tt, T.nf[:, 0:140], T.el[:, 0:140], T.j8[:, 0:140], A.not_equal)
        op("v", ["nf", "lst"], ["pen"], ts, T.pen[:], T.nf[:, 0:336].indirect(T.lst[:, 0:12]), 1024.0, None, A.mult)
        op("v", ["el", "el7", "pen"], ["pa0"], tt, T.pa[:, 0:160], T.el[:, 0:160], T.pen[:, 0:160], A.add)
        op("v", ["el", "el7", "pen"], ["pa1"], tt, T.pa[:, 160:320], T.el[:, 0:160], T.pen[:, 20:180], A.add)
        for src, dst, w in (("pa", "pb", 80), ("pb", "pc", 40), ("pc", "pd", 20)):
            for m in range(2):
                o = 2 * w * m
                op("v", [src + str(m)], [dst + str(m)], tt, T[dst][:, w * m:w * m + w], T[src][:, o:o + w], T[src][:, o + w:o + 2 * w], A.min)
        op("v", ["pd0", "pd1"], ["oab"], ts, T.oab[:], T.pd[:], 160.0, None, A.add)
        for b in range(4):
            op("s", ["fl%d" % b, "oab"], ["ga%d" % b], act, blk(T.ga, b), blk(T.fl, b).indirect(T.oab[:, 0:20]), AF.Copy)

        op("v", ["rs%d" % k for k in range(20)] + ["ec"], ["rk"], tt, T.rk[:], T.rs[:], T.ec[:, 15:320:16], A.subtract)
        op("v", ["rk"], ["rk16"], cp, T.rk16[:], T.rk[:])
        op("v", ["rk16", "tt"], ["ord"], cp, T.ord[:, 0:320].indirect(T.rk16[:, 0:20]), T.tt[:])
        op("v", ["ord", "m2"], ["lm"], tt, T.lm[:], T.ord[:, 0:128], T.m2[:, 0:128], A.min)
        op("v", ["lm", "res"], ["lsx"], sc, T.lsx[:], T.res[:, 0:128], T.lm[:], 0.0, A.add, A.max)
        op("v", ["lsx"], ["l16"], ts, T.l16[:], T.lsx[:, 15:128:16], 160.0, None, A.add)

        for b in range(4):
            op("v", ["fl%d" % b, "oab", "ga%d" % b], ["zp%d" % b], tt, blk(T.zp, b), blk(T.fl, b).indirect(T.oab[:, 20:40]), blk(T.ga, b), A.add)
        for b in range(4):
            if b % 2 == 0:
                op("s", ["zp%d" % b, "l16"], ["et%d" % b], act, T.et[:, b:512:4], blk(T.zp, b).indirect(T.l16[:, 0:8]), AF.Copy)
            else:
                op("v", ["zp%d" % b, "l16"], ["et%d" % b], cp, T.et[:, b:512:4], blk(T.zp, b).indirect(T.l16[:, 0:8]))
        EQ, ES, AQ, AS, arr = T["eq%d" % r], T["es%d" % r], T["aq%d" % r], T["as%d" % r], "arr%d" % r
        op("v", ["et0", "et1", "et2", "et3"], ["sent"], V.quantize_mx, EQ[:, 0:128], ES[:, 0:128], T.et[:])
        before("g", ["sent"], [])
        for out, in_ in ((AQ[:, 0:128].bitcast(dt.uint8), EQ[:, 0:128].bitcast(dt.uint8)), (AS[:, 0:128], ES[:, 0:128])):
            g.remote_dma(out_ap=out, in_ap=in_, remote_sem=T.sem[arr], local_sem=T.sem.loc, pid=pid, routing_id=rid, dma_engine_mask=mask)
        n = 2 * len(topo.engines(core, nxt))
        count["loc"] = count.get("loc", 0) + n
        count[arr] = n
        writer["came%d" % r] = (arr, n, {arr: n})

        op("v", ["rk"], ["ro16"], ts, T.ro16[:], T.rk[:], -191.0, 0.0, A.add, A.max)
        for n, (a, b) in enumerate(((0, 192), (128, 128), (192, 0))):
            w = 64 if a == b else 128
            op("v", ["ord"], ["ords%d" % n], cp, T.ords[:, a:a + w], T.ord[:, b:b + w])
        op("v", ["ords0", "ords1", "ords2", "rk16"], ["pi"], cp, T.pi[:], T.ords[:, 0:320].indirect(T.rk16[:, 0:20]))
        if r < ROUNDS - 1:
            op("v", ["pi", "cw16", "m2"], ["cm"], tt, T.cm[:], T.pi[:, 0:320].indirect(T.cw16[:, 0:20]), T.m2[:], A.min)
            op("v", ["cm", "res"], ["cs"], sc, T.cs[:], T.res[:], T.cm[:], 0.0, A.add, A.max)
            op("v", ["cs"], ["cw16"], ts, T.cw16[:], T.cs[:, 15:320:16], 160.0, None, A.add)
        else:
            op("v", ["pi", "cw16"], ["opl"], ts, T.opl[:], T.pi[:, 0:320].indirect(T.cw16[:, 0:20]), 160.0, None, A.add)
            dma("y", "out1", ["opl"], ["op"], T.op[:, :], T.opl[0:128:16, :])
        if r == 0:
            op("v", ["vt"], ["vq"], V.quantize_mx, T.vq[:, 0:128], T.vs[:, 0:128], T.vt[:])

        for b in range(4):
            mm("pf%d" % b, pf[b], 128, ["wq", "wsp"], blk(T.wq, b, 128), blk(T.wsp, b, 128), ["came%d" % r], AQ[:, 0:128], AS[:, 0:128])
        for b in range(4):
            op("s", ["pf%d" % b], ["rp%d" % b], act, T.rp[:, 136 * b + 1:136 * b + 129], pf[b][:, 0:128], AF.Copy, scale=0.03125)
        for b in range(4):
            op("v", ["rp%d" % b, "ro16", "zp%d" % b], ["x%d" % b], tt, T.xt[:, b:1280:4],
               T.rp[:, 136 * b:136 * b + 136].indirect(T.ro16[:, 0:20]), blk(T.zp, b), A.add)

    op("v", ["x0", "x1", "x2", "x3"], ["xq"], V.quantize_mx, T.xq[:, 0:320], T.xs[:, 0:320], T.xt[:])
    mm("py", T.py, 320, ["vq"], T.vq[:, 0:128], T.vs[:, 0:128], *QX)
    dma("y", "out1", ["xq"], ["oc"], T.oc[:, 0:1280], T.xq[:, 0:320].bitcast(dt.uint8))
    for k in range(4):
        q, s = (("s", "out2"), ("y", "out1"))[k % 2]
        dma(q, s, ["xq"], ["osc%d" % k], T.osc[4 * k:4 * k + 4, 0:320], T.xs[32 * k:32 * k + 4, 0:320])
    op("v", ["py"], ["yt"], cp, T.yt[:], T.py[:, 0:320])
    dma("s", "out2", ["yt"], ["y"], T.y[:], T.yt[:])
    for s in SEMAPHORES:
        if count.get(s, 0) and known["g"].get(s, 0) < count[s]:
            g.wait_ge(T.sem[s], count[s])
